import numpy as np, ml_dtypes
CORES = [72,74,76,78,200,202,204,206,328,330,332,334,456,458,460,462]
N = 16
G1 = [0,1,2,3,4,5,6,7,8,9,10,11,12,13,14,15]
G2 = [8,9,10,11,12,13,14,15]
def setup_inputs(rng):
    return {"x1": rng.standard_normal((N, 128, 512), dtype=np.float32), "x2": rng.standard_normal((N, 128, 4), dtype=np.float32).astype(ml_dtypes.bfloat16)}
def reference(x1, x2):
    out = {}
    y = np.full((N, 128, 512), np.nan, x1.dtype)
    s = x1[G1].sum(axis=0, dtype=np.float64).astype(x1.dtype)
    for r in G1:
        y[r] = s
    out["y1"] = y
    y = np.full((N, 128, 32), np.nan, x2.dtype)
    s = np.concatenate([x2[r] for r in G2], axis=1)
    for r in G2:
        y[r] = s
    out["y2"] = y
    return out

@@ -1,0 +1,112 @@
+from concourse.bass import DstId, RemoteDMATransfer
+
+NSIM = 512
+NP = 8
+PW = 64
+
+SCRATCH = {
+    "stage": ("dram", [NP, 128, PW], "float32"),
+    "acc": ("dram", [NP, 128, PW], "float32"),
+    "gat": ("sbuf", [128, 32], "bfloat16"),
+}
+SEMAPHORES = ["ld1", "ld2", "sent", "inq", "e1", "e2", "fin", "ag", "st1", "st2"]
+
+
+def _split(mask, k):
+    bits = [1 << b for b in range(mask.bit_length()) if (mask >> b) & 1]
+    n = len(bits) // k
+    return [sum(bits[i * n:(i + 1) * n]) for i in range(k)]
+
+
+def _count(mask):
+    return bin(mask).count("1")
+
+
+def _dst(topo, dst, src):
+    rid, pid = topo.addr(dst, src)
+    return DstId(rid=rid, pnc=pid)
+
+
+def rank_program(g, core, T, topo):
+    ranks = list(T.cores)
+    h = topo.host(core)
+    hosts = sorted({topo.host(c) for c in ranks})
+    rk = {x: [c for c in ranks if topo.host(c) == x] for x in hosts}
+    hp = {x: [c for c in range(NSIM) if topo.host(c) == x and topo.chip(c) == topo.chip(rk[x][0]) and c not in ranks]
+          for x in hosts}
+    if h not in hosts or (core not in rk[h] and core not in hp[h]):
+        return
+    S = T.sem
+
+    if core in hp[h]:
+        q = hp[h].index(core)
+        near = [hp[x][q] for x in hosts if x != h and topo.rack(x) == topo.rack(h)][0]
+        far = [hp[x][q] for x in hosts if topo.rack(x) != topo.rack(h) and topo.may_write(core, hp[x][q])][0]
+        ma, mb = _split(topo.mask(core, near) & topo.mask(core, far), 2)
+        a = [T.stage[i] for i in range(4)]
+        b = [T.stage[4 + i] for i in range(4)]
+        n_in = sum(2 * _count(_split(topo.mask(r, core), NP)[0]) for r in rk[h])
+
+        def xfer(srcs, dst, slot, mask, sem):
+            return RemoteDMATransfer(dst_ids=[_dst(topo, dst, core)], dma_engine_mask=mask, remote_sem=sem,
+                                     srcs=srcs, dsts=[T.acc[slot]], alu_op=1)
+
+        g.wait_ge(S.inq, n_in)
+        g.remote_dma_fused([xfer(a, near, 0, ma, S.e1), xfer(b, far, 1, mb, S.e1)], local_sem=S.sent)
+        g.wait_ge(S.e1, _count(ma) + _count(mb))
+        g.remote_dma_fused([xfer(a + [T.acc[0]], far, 2, ma, S.e2), xfer(b + [T.acc[1]], near, 3, mb, S.e2)],
+                           local_sem=S.sent)
+        g.wait_ge(S.e2, _count(ma) + _count(mb))
+        fa, fb = _split(topo.mask(core, rk[h][0]), 2)
+        ids = [_dst(topo, r, core) for r in rk[h]]
+        g.remote_dma_fused([
+            RemoteDMATransfer(dst_ids=ids, dma_engine_mask=fa, remote_sem=S.fin, srcs=a + [T.acc[0], T.acc[2]],
+                              dsts=[T.acc[q]] * len(ids), alu_op=1),
+            RemoteDMATransfer(dst_ids=ids, dma_engine_mask=fb, remote_sem=S.fin, srcs=b + [T.acc[1], T.acc[3]],
+                              dsts=[T.acc[4 + q]] * len(ids), alu_op=1),
+        ], local_sem=S.sent)
+        g.wait_ge(S.sent, 2 * (_count(ma) + _count(mb)) + _count(fa) + _count(fb))
+        return
+
+    i = rk[h].index(core)
+    rank = T.rank_of(core)
+    G2 = list(T.tables["G2"])
+    in2 = rank in G2
+    g.sync.dma_start(T.stage[:], T.x1[:]).then_inc(S.ld1, 16)
+    if in2:
+        j = G2.index(rank)
+        w = T.x2.shape[1]
+        mine = T.gat[:, w * j:w * (j + 1)]
+        g.scalar.dma_start(mine, T.x2[:]).then_inc(S.ld2, 16)
+
+    masks = _split(topo.mask(core, hp[h][0]), NP)
+    g.wait_ge(S.ld1, 16)
+    g.remote_dma_fused([
+        RemoteDMATransfer(dst_ids=[_dst(topo, hp[h][p % 4], core)], dma_engine_mask=masks[p], remote_sem=S.inq,
+                          src=T.stage[p], dst=T.stage[4 * (p // 4) + i])
+        for p in range(NP)], local_sem=S.sent)
+    sent = sum(_count(m) for m in masks)
+
+    if in2:
+        others = [ranks[r] for r in G2 if r != rank]
+        on = [c for c in others if topo.host(c) == h and topo.chip(c) == topo.chip(core)]
+        off = [c for c in others if c not in on]
+        m_off = topo.mask(core, off[0])
+        m_on = topo.mask(core, on[0]) & ~m_off
+        g.wait_ge(S.ld2, 16)
+        g.remote_dma_fused([
+            RemoteDMATransfer(dst_ids=[_dst(topo, c, core) for c in grp], dma_engine_mask=m, remote_sem=S.ag,
+                              srcs=[mine], dsts=[mine] * len(grp))
+            for grp, m in ((on, m_on), (off, m_off))], local_sem=S.sent)
+        sent += _count(m_on) + _count(m_off)
+        g.scalar.wait_ge(S.ld2, 16)
+        g.scalar.wait_ge(S.ag, len(on) * _count(m_on) + len(off) * _count(m_off))
+        g.scalar.dma_start(T.y2[:], T.gat[:]).then_inc(S.st2, 16)
+
+    n_fin = len(hp[h]) * _count(topo.mask(hp[h][0], core))
+    g.sync.wait_ge(S.fin, n_fin)
+    g.sync.dma_start(T.y1[:], T.acc[:]).then_inc(S.st1, 16)
+    g.wait_ge(S.sent, sent)
+    if in2:
+        g.wait_ge(S.st2, 16)
+    g.wait_ge(S.st1, 16)

@@ -9,7 +9,7 @@ SCRATCH = {
     "acc": ("dram", [NP, 128, PW], "float32"),
     "gat": ("sbuf", [128, 32], "bfloat16"),
 }
-SEMAPHORES = ["ld1", "ld2", "sent", "inq", "e1", "e2", "fin", "ag", "st1", "st2"]
+SEMAPHORES = ["ld2", "sent", "ag", "st2"] + [n + k for n in ("ld", "in", "e1", "e2", "fin", "st") for k in "ab"]
 
 
 def _split(mask, k):
@@ -37,55 +37,58 @@ def rank_program(g, core, T, topo):
     if h not in hosts or (core not in rk[h] and core not in hp[h]):
         return
     S = T.sem
+    halves = ((0, "a"), (1, "b"))
 
     if core in hp[h]:
         q = hp[h].index(core)
         near = [hp[x][q] for x in hosts if x != h and topo.rack(x) == topo.rack(h)][0]
         far = [hp[x][q] for x in hosts if topo.rack(x) != topo.rack(h) and topo.may_write(core, hp[x][q])][0]
-        ma, mb = _split(topo.mask(core, near) & topo.mask(core, far), 2)
-        a = [T.stage[i] for i in range(4)]
-        b = [T.stage[4 + i] for i in range(4)]
-        n_in = sum(2 * _count(_split(topo.mask(r, core), NP)[0]) for r in rk[h])
+        own = [[T.stage[4 * k + i] for i in range(4)] for k in (0, 1)]
+        n_in = sum(_count(_split(topo.mask(r, core), 4)[0]) for r in rk[h])
+        sent = 0
 
-        def xfer(srcs, dst, slot, mask, sem):
-            return RemoteDMATransfer(dst_ids=[_dst(topo, dst, core)], dma_engine_mask=mask, remote_sem=sem,
-                                     srcs=srcs, dsts=[T.acc[slot]], alu_op=1)
+        def fold(srcs, dsts, slot, sem):
+            m = topo.mask(core, dsts[0])
+            g.remote_dma_fused([RemoteDMATransfer(dst_ids=[_dst(topo, d, core) for d in dsts], dma_engine_mask=m,
+                                                  remote_sem=sem, srcs=srcs, dsts=[T.acc[slot]] * len(dsts), alu_op=1)],
+                               local_sem=S.sent)
+            return _count(m)
 
-        g.wait_ge(S.inq, n_in)
-        g.remote_dma_fused([xfer(a, near, 0, ma, S.e1), xfer(b, far, 1, mb, S.e1)], local_sem=S.sent)
-        g.wait_ge(S.e1, _count(ma) + _count(mb))
-        g.remote_dma_fused([xfer(a + [T.acc[0]], far, 2, ma, S.e2), xfer(b + [T.acc[1]], near, 3, mb, S.e2)],
-                           local_sem=S.sent)
-        g.wait_ge(S.e2, _count(ma) + _count(mb))
-        fa, fb = _split(topo.mask(core, rk[h][0]), 2)
-        ids = [_dst(topo, r, core) for r in rk[h]]
-        g.remote_dma_fused([
-            RemoteDMATransfer(dst_ids=ids, dma_engine_mask=fa, remote_sem=S.fin, srcs=a + [T.acc[0], T.acc[2]],
-                              dsts=[T.acc[q]] * len(ids), alu_op=1),
-            RemoteDMATransfer(dst_ids=ids, dma_engine_mask=fb, remote_sem=S.fin, srcs=b + [T.acc[1], T.acc[3]],
-                              dsts=[T.acc[4 + q]] * len(ids), alu_op=1),
-        ], local_sem=S.sent)
-        g.wait_ge(S.sent, 2 * (_count(ma) + _count(mb)) + _count(fa) + _count(fb))
+        for k, n in halves:
+            g.wait_ge(S["in" + n], n_in)
+            sent += fold(own[k], [(near, far)[k]], k, S["e1" + n])
+        for k, n in halves:
+            g.wait_ge(S["e1" + n], _count(topo.mask((near, far)[k], core)))
+            sent += fold(own[k] + [T.acc[k]], [(far, near)[k]], 2 + k, S["e2" + n])
+        for k, n in halves:
+            g.wait_ge(S["e2" + n], _count(topo.mask((far, near)[k], core)))
+            sent += fold(own[k] + [T.acc[k], T.acc[2 + k]], rk[h], 4 * k + q, S["fin" + n])
+        g.wait_ge(S.sent, sent)
         return
 
     i = rk[h].index(core)
     rank = T.rank_of(core)
     G2 = list(T.tables["G2"])
     in2 = rank in G2
-    g.sync.dma_start(T.stage[:], T.x1[:]).then_inc(S.ld1, 16)
+    rows = T.x1.shape[0] // 2
+    queue = (g.sync, g.scalar)
+    for k, n in halves:
+        queue[k].dma_start(T.stage[4 * k:4 * k + 4], T.x1[rows * k:rows * (k + 1), :]).then_inc(S["ld" + n], 16)
     if in2:
         j = G2.index(rank)
         w = T.x2.shape[1]
         mine = T.gat[:, w * j:w * (j + 1)]
         g.scalar.dma_start(mine, T.x2[:]).then_inc(S.ld2, 16)
 
-    masks = _split(topo.mask(core, hp[h][0]), NP)
-    g.wait_ge(S.ld1, 16)
-    g.remote_dma_fused([
-        RemoteDMATransfer(dst_ids=[_dst(topo, hp[h][p % 4], core)], dma_engine_mask=masks[p], remote_sem=S.inq,
-                          src=T.stage[p], dst=T.stage[4 * (p // 4) + i])
-        for p in range(NP)], local_sem=S.sent)
-    sent = sum(_count(m) for m in masks)
+    masks = _split(topo.mask(core, hp[h][0]), 4)
+    sent = 0
+    for k, n in halves:
+        g.wait_ge(S["ld" + n], 16)
+        g.remote_dma_fused([
+            RemoteDMATransfer(dst_ids=[_dst(topo, hp[h][q], core)], dma_engine_mask=masks[q], remote_sem=S["in" + n],
+                              src=T.stage[4 * k + q], dst=T.stage[4 * k + i])
+            for q in range(4)], local_sem=S.sent)
+        sent += sum(_count(m) for m in masks)
 
     if in2:
         others = [ranks[r] for r in G2 if r != rank]
@@ -104,9 +107,11 @@ def rank_program(g, core, T, topo):
         g.scalar.dma_start(T.y2[:], T.gat[:]).then_inc(S.st2, 16)
 
     n_fin = len(hp[h]) * _count(topo.mask(hp[h][0], core))
-    g.sync.wait_ge(S.fin, n_fin)
-    g.sync.dma_start(T.y1[:], T.acc[:]).then_inc(S.st1, 16)
+    for k, n in halves:
+        queue[k].wait_ge(S["fin" + n], n_fin)
+        queue[k].dma_start(T.y1[rows * k:rows * (k + 1), :], T.acc[4 * k:4 * k + 4]).then_inc(S["st" + n], 16)
     g.wait_ge(S.sent, sent)
     if in2:
         g.wait_ge(S.st2, 16)
-    g.wait_ge(S.st1, 16)
+    for k, n in halves:
+        g.wait_ge(S["st" + n], 16)

@@ -1,15 +1,15 @@
 from concourse.bass import DstId, RemoteDMATransfer
 
 NSIM = 512
-NP = 8
-PW = 64
+NC = 4
+PW = 512 // (4 * NC)
 
 SCRATCH = {
-    "stage": ("dram", [NP, 128, PW], "float32"),
-    "acc": ("dram", [NP, 128, PW], "float32"),
+    "stage": ("dram", [4 * NC, 128, PW], "float32"),
+    "acc": ("dram", [4 * NC, 128, PW], "float32"),
     "gat": ("sbuf", [128, 32], "bfloat16"),
 }
-SEMAPHORES = ["ld2", "sent", "ag", "st2"] + [n + k for n in ("ld", "in", "e1", "e2", "fin", "st") for k in "ab"]
+SEMAPHORES = ["ldg", "sent", "ag", "stg"] + ["%s%d" % (n, c) for n in ("ld", "in", "ea", "eb", "fin", "st") for c in range(NC)]
 
 
 def _split(mask, k):
@@ -37,15 +37,14 @@ def rank_program(g, core, T, topo):
     if h not in hosts or (core not in rk[h] and core not in hp[h]):
         return
     S = T.sem
-    halves = ((0, "a"), (1, "b"))
+    sent = 0
 
     if core in hp[h]:
         q = hp[h].index(core)
         near = [hp[x][q] for x in hosts if x != h and topo.rack(x) == topo.rack(h)][0]
         far = [hp[x][q] for x in hosts if topo.rack(x) != topo.rack(h) and topo.may_write(core, hp[x][q])][0]
-        own = [[T.stage[4 * k + i] for i in range(4)] for k in (0, 1)]
+        own = [[T.stage[4 * c + i] for i in range(4)] for c in range(NC)]
         n_in = sum(_count(_split(topo.mask(r, core), 4)[0]) for r in rk[h])
-        sent = 0
 
         def fold(srcs, dsts, slot, sem):
             m = topo.mask(core, dsts[0])
@@ -54,15 +53,15 @@ def rank_program(g, core, T, topo):
                                local_sem=S.sent)
             return _count(m)
 
-        for k, n in halves:
-            g.wait_ge(S["in" + n], n_in)
-            sent += fold(own[k], [(near, far)[k]], k, S["e1" + n])
-        for k, n in halves:
-            g.wait_ge(S["e1" + n], _count(topo.mask((near, far)[k], core)))
-            sent += fold(own[k] + [T.acc[k]], [(far, near)[k]], 2 + k, S["e2" + n])
-        for k, n in halves:
-            g.wait_ge(S["e2" + n], _count(topo.mask((far, near)[k], core)))
-            sent += fold(own[k] + [T.acc[k], T.acc[2 + k]], rk[h], 4 * k + q, S["fin" + n])
+        for c in range(NC):
+            g.wait_ge(S["in%d" % c], n_in)
+            sent += fold(own[c], [(near, far)[c % 2]], 2 * c, S["ea%d" % c])
+        for c in range(NC):
+            g.wait_ge(S["ea%d" % c], _count(topo.mask((near, far)[c % 2], core)))
+            sent += fold(own[c] + [T.acc[2 * c]], [(far, near)[c % 2]], 2 * c + 1, S["eb%d" % c])
+        for c in range(NC):
+            g.wait_ge(S["eb%d" % c], _count(topo.mask((far, near)[c % 2], core)))
+            sent += fold(own[c] + [T.acc[2 * c], T.acc[2 * c + 1]], rk[h], 4 * c + q, S["fin%d" % c])
         g.wait_ge(S.sent, sent)
         return
 
@@ -70,25 +69,29 @@ def rank_program(g, core, T, topo):
     rank = T.rank_of(core)
     G2 = list(T.tables["G2"])
     in2 = rank in G2
-    rows = T.x1.shape[0] // 2
+    rows = T.x1.shape[0] // NC
     queue = (g.sync, g.scalar)
-    for k, n in halves:
-        queue[k].dma_start(T.stage[4 * k:4 * k + 4], T.x1[rows * k:rows * (k + 1), :]).then_inc(S["ld" + n], 16)
+    for c in range(NC):
+        queue[c % 2].dma_start(T.stage[4 * c:4 * c + 4], T.x1[rows * c:rows * (c + 1), :]).then_inc(S["ld%d" % c], 16)
     if in2:
         j = G2.index(rank)
         w = T.x2.shape[1]
         mine = T.gat[:, w * j:w * (j + 1)]
-        g.scalar.dma_start(mine, T.x2[:]).then_inc(S.ld2, 16)
+        g.scalar.dma_start(mine, T.x2[:]).then_inc(S.ldg, 16)
 
     masks = _split(topo.mask(core, hp[h][0]), 4)
-    sent = 0
-    for k, n in halves:
-        g.wait_ge(S["ld" + n], 16)
+    for c in range(NC):
+        g.wait_ge(S["ld%d" % c], 16)
         g.remote_dma_fused([
-            RemoteDMATransfer(dst_ids=[_dst(topo, hp[h][q], core)], dma_engine_mask=masks[q], remote_sem=S["in" + n],
-                              src=T.stage[4 * k + q], dst=T.stage[4 * k + i])
+            RemoteDMATransfer(dst_ids=[_dst(topo, hp[h][q], core)], dma_engine_mask=masks[q], remote_sem=S["in%d" % c],
+                              src=T.stage[4 * c + q], dst=T.stage[4 * c + i])
             for q in range(4)], local_sem=S.sent)
         sent += sum(_count(m) for m in masks)
+
+    n_fin = len(hp[h]) * _count(topo.mask(hp[h][0], core))
+    for c in range(NC):
+        queue[c % 2].wait_ge(S["fin%d" % c], n_fin)
+        queue[c % 2].dma_start(T.y1[rows * c:rows * (c + 1), :], T.acc[4 * c:4 * c + 4]).then_inc(S["st%d" % c], 16)
 
     if in2:
         others = [ranks[r] for r in G2 if r != rank]
@@ -96,22 +99,15 @@ def rank_program(g, core, T, topo):
         off = [c for c in others if c not in on]
         m_off = topo.mask(core, off[0])
         m_on = topo.mask(core, on[0]) & ~m_off
-        g.wait_ge(S.ld2, 16)
+        g.wait_ge(S.ldg, 16)
         g.remote_dma_fused([
             RemoteDMATransfer(dst_ids=[_dst(topo, c, core) for c in grp], dma_engine_mask=m, remote_sem=S.ag,
                               srcs=[mine], dsts=[mine] * len(grp))
             for grp, m in ((on, m_on), (off, m_off))], local_sem=S.sent)
         sent += _count(m_on) + _count(m_off)
-        g.scalar.wait_ge(S.ld2, 16)
-        g.scalar.wait_ge(S.ag, len(on) * _count(m_on) + len(off) * _count(m_off))
-        g.scalar.dma_start(T.y2[:], T.gat[:]).then_inc(S.st2, 16)
-
-    n_fin = len(hp[h]) * _count(topo.mask(hp[h][0], core))
-    for k, n in halves:
-        queue[k].wait_ge(S["fin" + n], n_fin)
-        queue[k].dma_start(T.y1[rows * k:rows * (k + 1), :], T.acc[4 * k:4 * k + 4]).then_inc(S["st" + n], 16)
+        g.wait_ge(S.ag, len(on) * _count(m_on) + len(off) * _count(m_off))
+        g.dma_start(T.y2[:], T.gat[:]).then_inc(S.stg, 16)
+        g.wait_ge(S.stg, 16)
     g.wait_ge(S.sent, sent)
-    if in2:
-        g.wait_ge(S.st2, 16)
-    for k, n in halves:
-        g.wait_ge(S["st" + n], 16)
+    for c in range(NC):
+        g.wait_ge(S["st%d" % c], 16)

@@ -41,27 +41,30 @@ def rank_program(g, core, T, topo):
 
     if core in hp[h]:
         q = hp[h].index(core)
-        near = [hp[x][q] for x in hosts if x != h and topo.rack(x) == topo.rack(h)][0]
-        far = [hp[x][q] for x in hosts if topo.rack(x) != topo.rack(h) and topo.may_write(core, hp[x][q])][0]
-        own = [[T.stage[4 * c + i] for i in range(4)] for c in range(NC)]
+        bud = q + 1 if q % 2 == 0 else q - 1
+        near = [x for x in hosts if x != h and topo.rack(x) == topo.rack(h)][0]
+        far = [x for x in hosts if topo.rack(x) != topo.rack(h) and topo.may_write(core, hp[x][q])][0]
         n_in = sum(_count(_split(topo.mask(r, core), 4)[0]) for r in rk[h])
+        m_off = topo.mask(core, hp[near][bud]) & topo.mask(core, hp[far][bud]) & topo.mask(core, hp[h][bud])
 
-        def fold(srcs, dsts, slot, sem):
-            m = topo.mask(core, dsts[0])
-            g.remote_dma_fused([RemoteDMATransfer(dst_ids=[_dst(topo, d, core) for d in dsts], dma_engine_mask=m,
-                                                  remote_sem=sem, srcs=srcs, dsts=[T.acc[slot]] * len(dsts), alu_op=1)],
+        def fold(srcs, dsts, slots, mask, sem):
+            g.remote_dma_fused([RemoteDMATransfer(dst_ids=[_dst(topo, d, core) for d in dsts], dma_engine_mask=mask,
+                                                  remote_sem=sem, srcs=srcs, dsts=[T.acc[s] for s in slots], alu_op=1)],
                                local_sem=S.sent)
-            return _count(m)
+            return _count(mask)
 
         for c in range(NC):
             g.wait_ge(S["in%d" % c], n_in)
-            sent += fold(own[c], [(near, far)[c % 2]], 2 * c, S["ea%d" % c])
+            sent += fold([T.stage[4 * c + i] for i in range(4)], [hp[(near, far)[c % 2]][bud], hp[h][bud]],
+                         [4 * c + 1, 4 * c], m_off, S["ea%d" % c])
         for c in range(NC):
-            g.wait_ge(S["ea%d" % c], _count(topo.mask((near, far)[c % 2], core)))
-            sent += fold(own[c] + [T.acc[2 * c]], [(far, near)[c % 2]], 2 * c + 1, S["eb%d" % c])
+            g.wait_ge(S["ea%d" % c], 2 * _count(m_off))
+            sent += fold([T.acc[4 * c], T.acc[4 * c + 1]], [hp[(far, near)[c % 2]][bud], hp[h][bud]],
+                         [4 * c + 3, 4 * c + 2], m_off, S["eb%d" % c])
         for c in range(NC):
-            g.wait_ge(S["eb%d" % c], _count(topo.mask((far, near)[c % 2], core)))
-            sent += fold(own[c] + [T.acc[2 * c], T.acc[2 * c + 1]], rk[h], 4 * c + q, S["fin%d" % c])
+            g.wait_ge(S["eb%d" % c], 2 * _count(m_off))
+            sent += fold([T.acc[4 * c + 2], T.acc[4 * c + 3]], rk[h], [4 * c + q] * len(rk[h]),
+                         topo.mask(core, rk[h][0]), S["fin%d" % c])
         g.wait_ge(S.sent, sent)
         return
 

@@ -45,26 +45,27 @@ def rank_program(g, core, T, topo):
         near = [x for x in hosts if x != h and topo.rack(x) == topo.rack(h)][0]
         far = [x for x in hosts if topo.rack(x) != topo.rack(h) and topo.may_write(core, hp[x][q])][0]
         n_in = sum(_count(_split(topo.mask(r, core), 4)[0]) for r in rk[h])
-        m_off = topo.mask(core, hp[near][bud]) & topo.mask(core, hp[far][bud]) & topo.mask(core, hp[h][bud])
+        m_off = topo.mask(core, hp[near][bud]) & topo.mask(core, hp[far][bud])
+        m_on = topo.mask(core, hp[h][bud]) & ~m_off
 
-        def fold(srcs, dsts, slots, mask, sem):
+        def fold(srcs, parts, sem):
             g.remote_dma_fused([RemoteDMATransfer(dst_ids=[_dst(topo, d, core) for d in dsts], dma_engine_mask=mask,
-                                                  remote_sem=sem, srcs=srcs, dsts=[T.acc[s] for s in slots], alu_op=1)],
-                               local_sem=S.sent)
-            return _count(mask)
+                                                  remote_sem=sem, srcs=srcs, dsts=[T.acc[s] for s in slots], alu_op=1)
+                                for dsts, slots, mask in parts], local_sem=S.sent)
+            return sum(_count(mask) for dsts, slots, mask in parts)
 
         for c in range(NC):
             g.wait_ge(S["in%d" % c], n_in)
-            sent += fold([T.stage[4 * c + i] for i in range(4)], [hp[(near, far)[c % 2]][bud], hp[h][bud]],
-                         [4 * c + 1, 4 * c], m_off, S["ea%d" % c])
+            sent += fold([T.stage[4 * c + i] for i in range(4)],
+                         [([hp[(near, far)[c % 2]][bud]], [4 * c + 1], m_off), ([hp[h][bud]], [4 * c], m_on)], S["ea%d" % c])
         for c in range(NC):
-            g.wait_ge(S["ea%d" % c], 2 * _count(m_off))
-            sent += fold([T.acc[4 * c], T.acc[4 * c + 1]], [hp[(far, near)[c % 2]][bud], hp[h][bud]],
-                         [4 * c + 3, 4 * c + 2], m_off, S["eb%d" % c])
+            g.wait_ge(S["ea%d" % c], _count(m_off) + _count(m_on))
+            sent += fold([T.acc[4 * c], T.acc[4 * c + 1]],
+                         [([hp[(far, near)[c % 2]][bud]], [4 * c + 3], m_off), ([hp[h][bud]], [4 * c + 2], m_on)], S["eb%d" % c])
         for c in range(NC):
-            g.wait_ge(S["eb%d" % c], 2 * _count(m_off))
-            sent += fold([T.acc[4 * c + 2], T.acc[4 * c + 3]], rk[h], [4 * c + q] * len(rk[h]),
-                         topo.mask(core, rk[h][0]), S["fin%d" % c])
+            g.wait_ge(S["eb%d" % c], _count(m_off) + _count(m_on))
+            sent += fold([T.acc[4 * c + 2], T.acc[4 * c + 3]],
+                         [(rk[h], [4 * c + q] * len(rk[h]), topo.mask(core, rk[h][0]))], S["fin%d" % c])
         g.wait_ge(S.sent, sent)
         return
 

@@ -6,6 +6,7 @@ PW = 512 // (4 * NC)
 
 SCRATCH = {
     "stage": ("dram", [4 * NC, 128, PW], "float32"),
+    "mid": ("dram", [2 * NC, 128, PW], "float32"),
     "acc": ("dram", [4 * NC, 128, PW], "float32"),
     "gat": ("sbuf", [128, 32], "bfloat16"),
 }
@@ -38,34 +39,30 @@ def rank_program(g, core, T, topo):
         return
     S = T.sem
     sent = 0
+    near = [x for x in hosts if x != h and topo.rack(x) == topo.rack(h)][0]
+    far = [x for x in hosts if topo.rack(x) != topo.rack(h) and topo.may_write(core, rk[x][0])][0]
+    m_all = topo.mask(core, [c for c in rk[h] + hp[h] if c != core][0])
+    m_off = m_all & topo.mask(core, rk[near][0]) & topo.mask(core, rk[far][0])
+    m_on = m_all & ~m_off
+    n_two = _count(m_off) + _count(m_on)
+
+    def fold(srcs, parts, sem):
+        g.remote_dma_fused([RemoteDMATransfer(dst_ids=[_dst(topo, d, core) for d in dsts], dma_engine_mask=mask,
+                                              remote_sem=sem, srcs=srcs, dsts=aps, alu_op=1)
+                            for dsts, aps, mask in parts], local_sem=S.sent)
+        return sum(_count(mask) for dsts, aps, mask in parts)
 
     if core in hp[h]:
         q = hp[h].index(core)
-        bud = q + 1 if q % 2 == 0 else q - 1
-        near = [x for x in hosts if x != h and topo.rack(x) == topo.rack(h)][0]
-        far = [x for x in hosts if topo.rack(x) != topo.rack(h) and topo.may_write(core, hp[x][q])][0]
-        n_in = sum(_count(_split(topo.mask(r, core), 4)[0]) for r in rk[h])
-        m_off = topo.mask(core, hp[near][bud]) & topo.mask(core, hp[far][bud])
-        m_on = topo.mask(core, hp[h][bud]) & ~m_off
-
-        def fold(srcs, parts, sem):
-            g.remote_dma_fused([RemoteDMATransfer(dst_ids=[_dst(topo, d, core) for d in dsts], dma_engine_mask=mask,
-                                                  remote_sem=sem, srcs=srcs, dsts=[T.acc[s] for s in slots], alu_op=1)
-                                for dsts, slots, mask in parts], local_sem=S.sent)
-            return sum(_count(mask) for dsts, slots, mask in parts)
-
+        n_in = len(rk[h]) * _count(_split(m_all, 4)[0])
         for c in range(NC):
             g.wait_ge(S["in%d" % c], n_in)
             sent += fold([T.stage[4 * c + i] for i in range(4)],
-                         [([hp[(near, far)[c % 2]][bud]], [4 * c + 1], m_off), ([hp[h][bud]], [4 * c], m_on)], S["ea%d" % c])
+                         [([rk[(near, far)[c % 2]][q]], [T.mid[2 * c + 1]], m_off), ([rk[h][q]], [T.mid[2 * c]], m_on)],
+                         S["ea%d" % c])
         for c in range(NC):
-            g.wait_ge(S["ea%d" % c], _count(m_off) + _count(m_on))
-            sent += fold([T.acc[4 * c], T.acc[4 * c + 1]],
-                         [([hp[(far, near)[c % 2]][bud]], [4 * c + 3], m_off), ([hp[h][bud]], [4 * c + 2], m_on)], S["eb%d" % c])
-        for c in range(NC):
-            g.wait_ge(S["eb%d" % c], _count(m_off) + _count(m_on))
-            sent += fold([T.acc[4 * c + 2], T.acc[4 * c + 3]],
-                         [(rk[h], [4 * c + q] * len(rk[h]), topo.mask(core, rk[h][0]))], S["fin%d" % c])
+            g.wait_ge(S["eb%d" % c], n_two)
+            sent += fold([T.mid[2 * c], T.mid[2 * c + 1]], [(rk[h], [T.acc[4 * c + q]] * len(rk[h]), m_all)], S["fin%d" % c])
         g.wait_ge(S.sent, sent)
         return
 
@@ -83,7 +80,7 @@ def rank_program(g, core, T, topo):
         mine = T.gat[:, w * j:w * (j + 1)]
         g.scalar.dma_start(mine, T.x2[:]).then_inc(S.ldg, 16)
 
-    masks = _split(topo.mask(core, hp[h][0]), 4)
+    masks = _split(m_all, 4)
     for c in range(NC):
         g.wait_ge(S["ld%d" % c], 16)
         g.remote_dma_fused([
@@ -92,7 +89,7 @@ def rank_program(g, core, T, topo):
             for q in range(4)], local_sem=S.sent)
         sent += sum(_count(m) for m in masks)
 
-    n_fin = len(hp[h]) * _count(topo.mask(hp[h][0], core))
+    n_fin = len(hp[h]) * _count(m_all)
     for c in range(NC):
         queue[c % 2].wait_ge(S["fin%d" % c], n_fin)
         queue[c % 2].dma_start(T.y1[rows * c:rows * (c + 1), :], T.acc[4 * c:4 * c + 4]).then_inc(S["st%d" % c], 16)
@@ -101,14 +98,19 @@ def rank_program(g, core, T, topo):
         others = [ranks[r] for r in G2 if r != rank]
         on = [c for c in others if topo.host(c) == h and topo.chip(c) == topo.chip(core)]
         off = [c for c in others if c not in on]
-        m_off = topo.mask(core, off[0])
-        m_on = topo.mask(core, on[0]) & ~m_off
         g.wait_ge(S.ldg, 16)
         g.remote_dma_fused([
             RemoteDMATransfer(dst_ids=[_dst(topo, c, core) for c in grp], dma_engine_mask=m, remote_sem=S.ag,
                               srcs=[mine], dsts=[mine] * len(grp))
             for grp, m in ((on, m_on), (off, m_off))], local_sem=S.sent)
         sent += _count(m_on) + _count(m_off)
+
+    for c in range(NC):
+        g.wait_ge(S["ea%d" % c], n_two)
+        sent += fold([T.mid[2 * c], T.mid[2 * c + 1]],
+                     [([hp[(far, near)[c % 2]][i]], [T.mid[2 * c + 1]], m_off), ([hp[h][i]], [T.mid[2 * c]], m_on)], S["eb%d" % c])
+
+    if in2:
         g.wait_ge(S.ag, len(on) * _count(m_on) + len(off) * _count(m_off))
         g.dma_start(T.y2[:], T.gat[:]).then_inc(S.stg, 16)
         g.wait_ge(S.stg, 16)

from concourse.bass import DstId, RemoteDMATransfer

NSIM = 512
NC = 4
PW = 512 // (4 * NC)

SCRATCH = {
    "stage": ("dram", [4 * NC, 128, PW], "float32"),
    "mid": ("dram", [2 * NC, 128, PW], "float32"),
    "acc": ("dram", [4 * NC, 128, PW], "float32"),
    "gat": ("sbuf", [128, 32], "bfloat16"),
}
SEMAPHORES = ["ldg", "sent", "ag", "stg"] + ["%s%d" % (n, c) for n in ("ld", "in", "ea", "eb", "fin", "st") for c in range(NC)]


def _split(mask, k):
    bits = [1 << b for b in range(mask.bit_length()) if (mask >> b) & 1]
    n = len(bits) // k
    return [sum(bits[i * n:(i + 1) * n]) for i in range(k)]


def _count(mask):
    return bin(mask).count("1")


def _dst(topo, dst, src):
    rid, pid = topo.addr(dst, src)
    return DstId(rid=rid, pnc=pid)


def rank_program(g, core, T, topo):
    ranks = list(T.cores)
    h = topo.host(core)
    hosts = sorted({topo.host(c) for c in ranks})
    rk = {x: [c for c in ranks if topo.host(c) == x] for x in hosts}
    hp = {x: [c for c in range(NSIM) if topo.host(c) == x and topo.chip(c) == topo.chip(rk[x][0]) and c not in ranks]
          for x in hosts}
    if h not in hosts or (core not in rk[h] and core not in hp[h]):
        return
    S = T.sem
    sent = 0
    near = [x for x in hosts if x != h and topo.rack(x) == topo.rack(h)][0]
    far = [x for x in hosts if topo.rack(x) != topo.rack(h) and topo.may_write(core, rk[x][0])][0]
    m_all = topo.mask(core, [c for c in rk[h] + hp[h] if c != core][0])
    m_off = m_all & topo.mask(core, rk[near][0]) & topo.mask(core, rk[far][0])
    m_on = m_all & ~m_off
    n_two = _count(m_off) + _count(m_on)

    def fold(srcs, parts, sem):
        g.remote_dma_fused([RemoteDMATransfer(dst_ids=[_dst(topo, d, core) for d in dsts], dma_engine_mask=mask,
                                              remote_sem=sem, srcs=srcs, dsts=aps, alu_op=1)
                            for dsts, aps, mask in parts], local_sem=S.sent)
        return sum(_count(mask) for dsts, aps, mask in parts)

    if core in hp[h]:
        q = hp[h].index(core)
        n_in = len(rk[h]) * _count(_split(m_all, 4)[0])
        for c in range(NC):
            g.wait_ge(S["in%d" % c], n_in)
            sent += fold([T.stage[4 * c + i] for i in range(4)],
                         [([rk[(near, far)[c % 2]][q]], [T.mid[2 * c + 1]], m_off), ([rk[h][q]], [T.mid[2 * c]], m_on)],
                         S["ea%d" % c])
        for c in range(NC):
            g.wait_ge(S["eb%d" % c], n_two)
            sent += fold([T.mid[2 * c], T.mid[2 * c + 1]], [(rk[h], [T.acc[4 * c + q]] * len(rk[h]), m_all)], S["fin%d" % c])
        g.wait_ge(S.sent, sent)
        return

    i = rk[h].index(core)
    rank = T.rank_of(core)
    G2 = list(T.tables["G2"])
    in2 = rank in G2
    rows = T.x1.shape[0] // NC
    queue = (g.sync, g.scalar)
    for c in range(NC):
        queue[c % 2].dma_start(T.stage[4 * c:4 * c + 4], T.x1[rows * c:rows * (c + 1), :]).then_inc(S["ld%d" % c], 16)
    if in2:
        j = G2.index(rank)
        w = T.x2.shape[1]
        mine = T.gat[:, w * j:w * (j + 1)]
        g.scalar.dma_start(mine, T.x2[:]).then_inc(S.ldg, 16)

    masks = _split(m_all, 4)
    for c in range(NC):
        g.wait_ge(S["ld%d" % c], 16)
        g.remote_dma_fused([
            RemoteDMATransfer(dst_ids=[_dst(topo, hp[h][q], core)], dma_engine_mask=masks[q], remote_sem=S["in%d" % c],
                              src=T.stage[4 * c + q], dst=T.stage[4 * c + i])
            for q in range(4)], local_sem=S.sent)
        sent += sum(_count(m) for m in masks)

    n_fin = len(hp[h]) * _count(m_all)
    for c in range(NC):
        queue[c % 2].wait_ge(S["fin%d" % c], n_fin)
        queue[c % 2].dma_start(T.y1[rows * c:rows * (c + 1), :], T.acc[4 * c:4 * c + 4]).then_inc(S["st%d" % c], 16)

    if in2:
        others = [ranks[r] for r in G2 if r != rank]
        on = [c for c in others if topo.host(c) == h and topo.chip(c) == topo.chip(core)]
        off = [c for c in others if c not in on]
        g.wait_ge(S.ldg, 16)
        g.remote_dma_fused([
            RemoteDMATransfer(dst_ids=[_dst(topo, c, core) for c in grp], dma_engine_mask=m, remote_sem=S.ag,
                              srcs=[mine], dsts=[mine] * len(grp))
            for grp, m in ((on, m_on), (off, m_off))], local_sem=S.sent)
        sent += _count(m_on) + _count(m_off)

    for c in range(NC):
        g.wait_ge(S["ea%d" % c], n_two)
        sent += fold([T.mid[2 * c], T.mid[2 * c + 1]],
                     [([hp[(far, near)[c % 2]][i]], [T.mid[2 * c + 1]], m_off), ([hp[h][i]], [T.mid[2 * c]], m_on)], S["eb%d" % c])

    if in2:
        g.wait_ge(S.ag, len(on) * _count(m_on) + len(off) * _count(m_off))
        g.dma_start(T.y2[:], T.gat[:]).then_inc(S.stg, 16)
        g.wait_ge(S.stg, 16)
    g.wait_ge(S.sent, sent)
    for c in range(NC):
        g.wait_ge(S["st%d" % c], 16)
